import numpy as np
import ml_dtypes


def mxq(x, axis, fmt="e4m3"):
    dtype, down = {"e4m3": (ml_dtypes.float8_e4m3fn, 7), "e5m2": (ml_dtypes.float8_e5m2, 14)}[fmt]
    v = np.moveaxis(np.asarray(x, np.float32).astype(ml_dtypes.bfloat16).astype(np.float64), axis, -1)
    blocks = v.reshape(v.shape[:-1] + (-1, 32))
    amax = np.abs(blocks).max(-1, keepdims=True)
    byte = np.maximum(np.where(amax > 0, np.frexp(amax)[1] - 1 + 127, 0) - down, 1)
    scale = np.exp2(byte - 127.0)
    codes = (blocks / scale).astype(np.float32).astype(dtype).astype(np.float64)
    return np.moveaxis((codes * scale).reshape(v.shape), -1, axis)


WIDE = False


def mx_kscale(k):
    if not WIDE:
        return np.ones(k)
    levels = np.array([10, -10, 5, -5, 0])
    if k % 512:
        return np.exp2(np.random.permutation(np.resize(levels, k // 32))).repeat(32)
    a = np.empty((k // 512, 16))
    for p in range(k // 512):
        a[p, :8] = np.random.permutation(np.resize(levels, 8))
        for g in range(8):
            far = levels[np.abs(levels - a[p, g]) >= 10]
            a[p, g + 8] = far[np.random.randint(len(far))]
    return np.exp2(a.ravel()).repeat(32)


def f64(x):
    return np.asarray(x).astype(np.float64)


E2M1 = np.array([0.0, 0.5, 1.0, 1.5, 2.0, 3.0, 4.0, 6.0, -0.0, -0.5, -1.0, -1.5, -2.0, -3.0, -4.0, -6.0])


def pack_weight(w, fmt):
    k, n = w.shape
    w = f64(np.asarray(w, np.float32).astype(ml_dtypes.bfloat16)).reshape(k // 32, 32, n)
    amax = np.abs(w).max(1)
    if fmt == "e4m3":
        byte = np.frexp(amax)[1] - 1 + 127 - 7
    else:
        mant, ex = np.frexp(amax / 6.0)
        byte = np.where(mant > 0.5, ex, ex - 1) + 127
    byte = np.clip(np.where(amax > 0, byte, 1), 1, 254)
    scaled = (w * np.exp2(127.0 - byte)[:, None, :]).reshape(k, n).astype(np.float32)
    by_word = np.ascontiguousarray(scaled.reshape(k // 512, 128, 4, n).transpose(0, 1, 3, 2))
    if fmt == "e4m3":
        words = by_word.astype(ml_dtypes.float8_e4m3fn).view(np.uint8)
    else:
        c = by_word.astype(ml_dtypes.float4_e2m1fn).view(np.uint8) & 0xF
        words = (c[..., 0::2] | (c[..., 1::2] << 4)).reshape(k // 512, 128, 2 * n)
    return np.ascontiguousarray(words), np.ascontiguousarray(byte.astype(np.uint8).reshape(k // 512, 16, n))


def unpack_weight(words, scales, fmt):
    g, _, n = scales.shape
    words = np.ascontiguousarray(words).reshape(g, 128, n, -1)
    if fmt == "e4m3":
        vals = words.view(ml_dtypes.float8_e4m3fn).astype(np.float64)
    else:
        nib = np.empty((g, 128, n, 4), np.uint8)
        nib[..., 0::2] = words & 0xF
        nib[..., 1::2] = words >> 4
        vals = E2M1[nib]
    vals = vals * np.repeat(np.exp2(scales.astype(np.float64) - 127.0), 8, axis=1)[..., None]
    return vals.transpose(0, 1, 3, 2).reshape(g * 512, n)


def bf(x):
    return np.asarray(x, np.float32).astype(ml_dtypes.bfloat16)


def planes(Y):
    r, m = Y.shape
    b = f64(bf(Y)).reshape(r // 32, 32, m)
    amax = np.abs(b).max(1)
    byte = np.clip(np.where(amax > 0, np.frexp(amax)[1] - 1 + 127 - 7, 1), 1, 254)
    codes = (b * np.exp2(127.0 - byte)[:, None, :]).reshape(r, m).astype(np.float32).astype(ml_dtypes.float8_e4m3fn).view(np.uint8)
    words = codes.reshape(r // 512, 128, 4, m).transpose(0, 1, 3, 2)
    return np.ascontiguousarray(words), np.ascontiguousarray(byte.astype(np.uint8).reshape(r // 512, 16, m))


K, L, T, N = 1024, 1024, 512, 512


def setup_inputs():
    n = np.random.standard_normal
    fk = mx_kscale(K)
    fl = mx_kscale(L)
    wap = pack_weight(n((K, N)) * 1 / np.sqrt(K) * fk[:, None], "e2m1")
    xqp = pack_weight(n((L, T)) / fl[:, None], "e4m3")
    wqp = pack_weight(n((L, N)) * 1 / np.sqrt(L) * fl[:, None], "e2m1")
    wcp = pack_weight(n((L, N)) * 1 / np.sqrt(L) * fl[:, None], "e4m3")
    return {
        "xt": (n((K, T)) / fk[:, None]).astype(np.float32),
        "wa_words": wap[0],
        "wa_scales": wap[1],
        "xq_words": xqp[0],
        "xq_scales": xqp[1],
        "wq_words": wqp[0],
        "wq_scales": wqp[1],
        "wb": (n((K, N)) * 1 / np.sqrt(K) * fk[:, None]).astype(np.float32),
        "wc_words": wcp[0],
        "wc_scales": wcp[1],
    }


def reference(xt, wa_words, wa_scales, xq_words, xq_scales, wq_words, wq_scales, wb, wc_words, wc_scales):
    wau = unpack_weight(wa_words, wa_scales, "e2m1")
    xqu = unpack_weight(xq_words, xq_scales, "e4m3")
    wqu = unpack_weight(wq_words, wq_scales, "e2m1")
    wcu = unpack_weight(wc_words, wc_scales, "e4m3")
    xtq = mxq(f64(xt), 0, "e4m3")
    p = wau.T @ xtq + wqu.T @ xqu
    wbq = mxq(f64(wb), 0, "e4m3")
    r = wbq.T @ xtq
    s = wcu.T @ xqu
    lo = np.minimum(r, s)
    hi = np.maximum(r, s)
    y = np.maximum(lo, np.minimum(hi, 0.7 * p))
    words, scales = planes(y)
    return y, words, scales

@@ -1,0 +1,330 @@
+from contextlib import ExitStack
+
+import concourse.mybir as mybir
+from concourse.masks import make_identity
+
+K, L, T, N = 1024, 1024, 512, 512
+FLOPS = 2 * N * T * (2 * K + 2 * L)
+
+F32 = mybir.dt.float32
+BF16 = mybir.dt.bfloat16
+I32 = mybir.dt.int32
+U32 = mybir.dt.uint32
+U8 = mybir.dt.uint8
+FP8X4 = mybir.dt.float8_e4m3fn_x4
+FP4X4 = mybir.dt.float4_e2m1fn_x4
+ALU = mybir.AluOpType
+
+P = 128
+PACK = 4
+PASSES = 2
+CHUNKS = 4
+HALF = 256
+P_FACTOR = 0.7
+
+
+def tile_mix_three_sums_middle_pl_kernel(
+    tc, xt, wa_words, wa_scales, xq_words, xq_scales, wq_words, wq_scales, wb, wc_words, wc_scales,
+    out_0, out_1, out_2,
+):
+    nc = tc.nc
+    with ExitStack() as ctx:
+        sb = ctx.enter_context(tc.tile_pool(name="sb", bufs=1))
+        ps = ctx.enter_context(tc.psum_pool(name="ps", bufs=1))
+        ctx.enter_context(tc.manual_schedule())
+
+        def sbuf(name, shape, dtype):
+            return sb.tile(shape, dtype, name=name, align_bytes=64)
+
+        def bank(tag, name, shape):
+            return ps.tile(shape, F32, name=name, tag=tag)
+
+        wc_c = sbuf("wc_c", [P, PASSES, N], U32)
+        xq_c = sbuf("xq_c", [P, PASSES, T], U32)
+        wq_c = sbuf("wq_c", [P, PASSES, 2 * N], U8)
+        wa_c = sbuf("wa_c", [P, PASSES, 2 * N], U8)
+        xq_s = sbuf("xq_s", [P, PASSES, T], U8)
+        wc_s = sbuf("wc_s", [P, PASSES, N], U8)
+        wq_s = sbuf("wq_s", [P, PASSES, N], U8)
+        wa_s = sbuf("wa_s", [P, PASSES, N], U8)
+        ident = sbuf("ident", [P, P], F32)
+
+        x_raw = [[sbuf("x_raw%d%d" % (c, g), [P, PACK, P], F32) for g in range(PASSES)] for c in range(CHUNKS)]
+        x_bf = [sbuf("x_bf%d" % c, [P, PASSES, P, PACK], BF16) for c in range(CHUNKS)]
+        x_c = [sbuf("x_c%d" % c, [P, PASSES, P], U32) for c in range(CHUNKS)]
+        x_s = [sbuf("x_s%d" % c, [P, PASSES, P], U8) for c in range(CHUNKS)]
+        w_raw = [[sbuf("w_raw%d%d" % (h, g), [P, PACK, HALF], F32) for g in range(PASSES)] for h in range(2)]
+        w_bf = [[sbuf("w_bf%d%d" % (h, g), [P, HALF, PACK], BF16) for g in range(PASSES)] for h in range(2)]
+        w_c = [sbuf("w_c%d" % h, [P, PASSES, HALF], U32) for h in range(2)]
+        w_s = [sbuf("w_s%d" % h, [P, PASSES, HALF], U8) for h in range(2)]
+
+        s_sb = [sbuf("s_sb%d" % c, [P, PACK, P], F32) for c in range(CHUNKS)]
+        lo = [sbuf("lo%d" % a, [P, PACK, 2, P], F32) for a in range(2)]
+        hi = [sbuf("hi%d" % a, [P, PACK, 2, P], F32) for a in range(2)]
+        capped = [[sbuf("capped%d%d" % (h, a), [P, PACK, 2, 64], F32) for a in range(2)] for h in range(2)]
+        y_t = [[sbuf("y_t%d%d" % (h, a), [P, PACK, 2, 64], F32) for a in range(2)] for h in range(2)]
+        y_sb = [[sbuf("y_sb%d%d" % (h, a), [P, PACK, P], F32) for a in range(2)] for h in range(2)]
+        y_bf = [[sbuf("y_bf%d%d" % (h, a), [P, P, PACK], BF16) for a in range(2)] for h in range(2)]
+        y_c = [sbuf("y_c%d" % h, [P, 2, P], U32) for h in range(2)]
+        y_s = sbuf("y_s", [P, 2, 2, P], U8)
+
+        nc.gpsimd.memset(wq_s[:].bitcast(I32), 0)
+        for plane in (wa_s, xq_s, wc_s):
+            nc.vector.memset(plane[:].bitcast(I32), 0)
+
+        def load_words(dst, words):
+            nc.sync.dma_start(out=dst[:].bitcast(I32), in_=words.bitcast(I32))
+
+        def load_scales(queue, plane, scales):
+            for q in range(4):
+                queue.dma_start(
+                    out=plane[32 * q : 32 * q + 4].bitcast(I32),
+                    in_=scales[:, 4 * q : 4 * q + 4, :].rearrange("g i n -> i g n").bitcast(I32),
+                )
+
+        def first_token(c):
+            return HALF * (c % 2) + P * (c // 2)
+
+        def load_rows(raw, src, g, col0):
+            rows = src[512 * g : 512 * (g + 1), col0 : col0 + raw.shape[2]]
+            nc.sync.dma_start(out=raw[:], in_=rows.rearrange("(p j) w -> p j w", j=PACK))
+
+        def load_x(c, g):
+            load_rows(x_raw[c][g], xt, g, first_token(c))
+
+        def load_w(h, g):
+            load_rows(w_raw[h][g], wb, g, HALF * h)
+
+        load_scales(nc.gpsimd, wq_s, wq_scales)
+        make_identity(nc, ident[:])
+        load_x(0, 0)
+        load_scales(nc.sync, wa_s, wa_scales)
+        load_x(0, 1)
+        load_words(wa_c, wa_words.rearrange("g p n -> p g n"))
+        load_x(1, 0)
+        load_scales(nc.sync, xq_s, xq_scales)
+        load_x(1, 1)
+        load_words(xq_c, xq_words.rearrange("g p n t -> p g (n t)"))
+        load_words(wc_c, wc_words.rearrange("g p n t -> p g (n t)"))
+        load_scales(nc.sync, wc_s, wc_scales)
+        load_words(wq_c, wq_words.rearrange("g p n -> p g n"))
+        for load, blocks in ((load_x, (2, 3)), (load_w, (0, 1))):
+            for i in blocks:
+                for g in range(PASSES):
+                    load(i, g)
+
+        def copy(engine, out, in_):
+            if engine == "scalar":
+                nc.scalar.copy(out=out, in_=in_)
+            else:
+                nc.vector.tensor_copy(out=out, in_=in_)
+
+        def round_block(engine, grouped, raw):
+            copy(engine, grouped.rearrange("p (c i) j -> p c j i", i=4), raw.rearrange("p j (c i) -> p c j i", i=4))
+
+        def round_x(engine, c, g):
+            round_block(engine, x_bf[c][:, g], x_raw[c][g][:])
+
+        def round_w(engine, h, g, b):
+            cols = slice(P * b, P * (b + 1))
+            round_block(engine, w_bf[h][g][:, cols, :], w_raw[h][g][:, :, cols])
+
+        def quantize(grouped, codes, scales):
+            nc.vector.quantize_mx(out=codes.bitcast(FP8X4), scales=scales, in_=grouped)
+
+        def quantize_x(c):
+            quantize(
+                x_bf[c][:].rearrange("p g w j -> p (g w j)"),
+                x_c[c][:].rearrange("p g w -> p (g w)"),
+                x_s[c][:].rearrange("p g w -> p (g w)"),
+            )
+
+        def quantize_w(h, g):
+            quantize(w_bf[h][g][:].rearrange("p w j -> p (w j)"), w_c[h][:, g, :], w_s[h][:, g, :])
+
+        def xq_product(acc, c, w_codes, w_dtype, w_scales, start, stop):
+            cols = slice(first_token(c), first_token(c) + P)
+            for g in range(PASSES):
+                nc.tensor.matmul_mx(
+                    out=acc, lhsT=xq_c[:, g, cols].bitcast(FP8X4), lhsT_scale=xq_s[:, g, cols],
+                    rhs=w_codes[:, g, :].bitcast(w_dtype), rhs_scale=w_scales[:, g, :],
+                    start=start and g == 0, stop=stop and g == PASSES - 1,
+                )
+
+        def xt_product(acc, c, w_codes, w_dtype, w_scales, start, stop):
+            for g in range(PASSES):
+                nc.tensor.matmul_mx(
+                    out=acc, lhsT=x_c[c][:, g, :].bitcast(FP8X4), lhsT_scale=x_s[c][:, g, :],
+                    rhs=w_codes[:, g, :].bitcast(w_dtype), rhs_scale=w_scales[:, g, :],
+                    start=start and g == 0, stop=stop and g == PASSES - 1,
+                )
+
+        s_ps, p_ps, r_ps = {}, {}, {}
+
+        def s_mm(c):
+            s_ps[c] = bank("u%d" % c, "s_ps%d" % c, [P, N])
+            xq_product(s_ps[c][:], c, wc_c, FP8X4, wc_s, True, True)
+
+        def s_out(engine, c):
+            copy(engine, s_sb[c][:], s_ps[c][:].rearrange("t (m r) -> t r m", r=PACK))
+
+        def p_open(c):
+            p_ps[c] = bank("v%d" % c, "p_ps%d" % c, [P, N])
+            xt_product(p_ps[c][:], c, wa_c, FP4X4, wa_s, True, False)
+
+        def p_close(c):
+            xq_product(p_ps[c][:], c, wq_c, FP4X4, wq_s, False, True)
+
+        def p_open_late(c):
+            p_ps[c] = bank("v%d" % c, "p_ps%d" % c, [P, N])
+            xq_product(p_ps[c][:], c, wq_c, FP4X4, wq_s, True, False)
+
+        def p_close_late(c):
+            xt_product(p_ps[c][:], c, wa_c, FP4X4, wa_s, False, True)
+
+        def bound(dst, c, op):
+            nc.vector.scalar_tensor_tensor(
+                out=dst[c // 2][:, :, c % 2, :], in0=p_ps[c][:].rearrange("t (m r) -> t r m", r=PACK),
+                scalar=P_FACTOR, in1=s_sb[c][:], op0=ALU.mult, op1=op,
+            )
+
+        def r_mm(h, a, tag):
+            r_ps[h, a] = bank(tag, "r_ps%d%d" % (h, a), [P, 2, HALF])
+            for g in range(PASSES):
+                for cc in range(2):
+                    c = 2 * a + cc
+                    nc.tensor.matmul_mx(
+                        out=r_ps[h, a][:, cc, :], lhsT=x_c[c][:, g, :].bitcast(FP8X4), lhsT_scale=x_s[c][:, g, :],
+                        rhs=w_c[h][:, g, :].bitcast(FP8X4), rhs_scale=w_s[h][:, g, :],
+                        start=g == 0 and cc == 0, stop=g == PASSES - 1 and cc == 1,
+                    )
+
+        def cap(h, a, rows):
+            nc.vector.tensor_tensor(
+                out=capped[h][a][:, rows], in0=r_ps[h, a][:].rearrange("t c (m r) -> t r c m", r=PACK)[:, rows],
+                in1=hi[a][:, rows, :, 64 * h : 64 * (h + 1)], op=ALU.min,
+            )
+
+        def floor(h, a, rows):
+            nc.vector.tensor_tensor(
+                out=y_t[h][a][:, rows], in0=capped[h][a][:, rows],
+                in1=lo[a][:, rows, :, 64 * h : 64 * (h + 1)], op=ALU.max,
+            )
+
+        def clamp(h, a):
+            for step in (cap, floor):
+                for r0 in (0, 2):
+                    step(h, a, slice(r0, r0 + 2))
+
+        def turn(h, a, tag):
+            turned = bank(tag, "t_ps%d%d%s" % (h, a, tag), [P, PACK, P])
+            for r in range(PACK):
+                nc.tensor.transpose(turned[:, r, :], y_t[h][a][:, r].rearrange("t c m -> t (c m)"), ident[:])
+            return turned
+
+        def y_out(turned, h, a):
+            nc.scalar.copy(out=y_sb[h][a][:], in_=turned[:])
+
+        def y_round(engine, turned, h, a):
+            copy(engine, y_bf[h][a][:], turned[:].rearrange("p r t -> p t r"))
+
+        def y_quantize(h, a):
+            quantize(y_bf[h][a][:].rearrange("p t r -> p (t r)"), y_c[h][:, a, :], y_s[:, h, a, :])
+
+        def store_values(queue, h, a):
+            for cc in range(2):
+                t0 = first_token(2 * a + cc)
+                rows = out_0[HALF * h : HALF * (h + 1), t0 : t0 + P]
+                queue.dma_start(out=rows.rearrange("(p r) t -> p r t", r=PACK), in_=y_sb[h][a][64 * cc : 64 * (cc + 1)])
+
+        def store_words(h):
+            words = out_1[0].rearrange("p t r -> p (t r)").bitcast(I32)
+            for cc in range(2):
+                nc.sync.dma_start(
+                    out=words[64 * h : 64 * (h + 1), HALF * cc : HALF * (cc + 1)],
+                    in_=y_c[h][64 * cc : 64 * (cc + 1)].rearrange("p a t -> p (a t)").bitcast(I32),
+                )
+
+        def store_scales():
+            rows = out_2[0].rearrange("(h b i) t -> b i h t", h=2, b=2)
+            for q in range(4):
+                cc, b = divmod(q, 2)
+                (nc.sync, nc.scalar)[b].dma_start(
+                    out=rows[b][:, :, HALF * cc : HALF * (cc + 1)].bitcast(I32),
+                    in_=y_s[32 * q : 32 * q + 4].rearrange("i h a t -> i h (a t)").bitcast(I32),
+                )
+
+        def post(h, a):
+            turned = turn(h, a, "v%d" % (2 * h + a))
+            y_out(turned, h, a)
+            store_values(nc.sync, h, a)
+            y_round(S, turned, h, a)
+
+        S, V = "scalar", "vector"
+        for c in range(2):
+            round_x(S, c, 0)
+            round_x(V, c, 1)
+            quantize_x(c)
+            p_open(c)
+        s_mm(0)
+        s_out(S, 0)
+        round_x(V, 2, 0)
+        p_close(0)
+        s_mm(1)
+        p_close(1)
+        round_x(S, 2, 1)
+        s_out(S, 1)
+        bound(hi, 0, ALU.max)
+        bound(lo, 0, ALU.min)
+        quantize_x(2)
+        s_mm(2)
+        p_open_late(2)
+        p_close_late(2)
+        round_x(S, 3, 0)
+        s_out(S, 2)
+        round_x(S, 3, 1)
+        bound(hi, 1, ALU.max)
+        bound(lo, 1, ALU.min)
+        bound(hi, 2, ALU.max)
+        quantize_x(3)
+        s_mm(3)
+        p_open_late(3)
+        p_close_late(3)
+        s_out(S, 3)
+        bound(lo, 2, ALU.min)
+        round_w(V, 0, 0, 0)
+        round_w(S, 0, 0, 1)
+        round_w(S, 0, 1, 0)
+        round_w(S, 0, 1, 1)
+        bound(hi, 3, ALU.max)
+        quantize_w(0, 0)
+        quantize_w(0, 1)
+        r_mm(0, 0, "u0")
+        r_mm(0, 1, "u1")
+        bound(lo, 3, ALU.min)
+        for g in range(PASSES):
+            for b in range(2):
+                round_w(S, 1, g, b)
+        clamp(0, 0)
+        post(0, 0)
+        for g in range(PASSES):
+            quantize_w(1, g)
+        r_mm(1, 0, "u2")
+        r_mm(1, 1, "u3")
+        clamp(0, 1)
+        post(0, 1)
+        clamp(1, 0)
+        post(1, 0)
+        clamp(1, 1)
+        last_for_planes = turn(1, 1, "v3")
+        last_for_values = turn(1, 1, "u0")
+        y_quantize(0, 0)
+        y_quantize(0, 1)
+        store_words(0)
+        y_round(V, last_for_planes, 1, 1)
+        y_out(last_for_values, 1, 1)
+        store_values(nc.scalar, 1, 1)
+        y_quantize(1, 0)
+        y_quantize(1, 1)
+        store_words(1)
+        store_scales()

@@ -1,7 +1,6 @@
 from contextlib import ExitStack
 
 import concourse.mybir as mybir
-from concourse.masks import make_identity
 
 K, L, T, N = 1024, 1024, 512, 512
 FLOPS = 2 * N * T * (2 * K + 2 * L)
@@ -39,37 +38,41 @@ def tile_mix_three_sums_middle_pl_kernel(
         def bank(tag, name, shape):
             return ps.tile(shape, F32, name=name, tag=tag)
 
-        wc_c = sbuf("wc_c", [P, PASSES, N], U32)
-        xq_c = sbuf("xq_c", [P, PASSES, T], U32)
-        wq_c = sbuf("wq_c", [P, PASSES, 2 * N], U8)
-        wa_c = sbuf("wa_c", [P, PASSES, 2 * N], U8)
+        wc_in = sbuf("wc_in", [P, PASSES, N], I32)
+        wq_in = sbuf("wq_in", [P, PASSES, 2 * N], U8)
+        wa_in = sbuf("wa_in", [P, PASSES, 2 * N], U8)
+        wc_s_in = sbuf("wc_s_in", [P, N], U8)
+        wq_s_in = sbuf("wq_s_in", [P, PASSES, N], U8)
+        wa_s_in = sbuf("wa_s_in", [P, PASSES, N], U8)
+        wc_c = sbuf("wc_c", [P, PASSES, PACK, P], I32)
+        wq_c = sbuf("wq_c", [P, PASSES, PACK, 2 * P], U8)
+        wa_c = sbuf("wa_c", [P, PASSES, PACK, 2 * P], U8)
+        wc_s = sbuf("wc_s", [P, PACK, P], U8)
+        wq_s = sbuf("wq_s", [P, PASSES, PACK, P], U8)
+        wa_s = sbuf("wa_s", [P, PASSES, PACK, P], U8)
+        xq_c = sbuf("xq_c", [P, PASSES, T], I32)
         xq_s = sbuf("xq_s", [P, PASSES, T], U8)
-        wc_s = sbuf("wc_s", [P, PASSES, N], U8)
-        wq_s = sbuf("wq_s", [P, PASSES, N], U8)
-        wa_s = sbuf("wa_s", [P, PASSES, N], U8)
-        ident = sbuf("ident", [P, P], F32)
 
-        x_raw = [[sbuf("x_raw%d%d" % (c, g), [P, PACK, P], F32) for g in range(PASSES)] for c in range(CHUNKS)]
-        x_bf = [sbuf("x_bf%d" % c, [P, PASSES, P, PACK], BF16) for c in range(CHUNKS)]
-        x_c = [sbuf("x_c%d" % c, [P, PASSES, P], U32) for c in range(CHUNKS)]
-        x_s = [sbuf("x_s%d" % c, [P, PASSES, P], U8) for c in range(CHUNKS)]
-        w_raw = [[sbuf("w_raw%d%d" % (h, g), [P, PACK, HALF], F32) for g in range(PASSES)] for h in range(2)]
-        w_bf = [[sbuf("w_bf%d%d" % (h, g), [P, HALF, PACK], BF16) for g in range(PASSES)] for h in range(2)]
-        w_c = [sbuf("w_c%d" % h, [P, PASSES, HALF], U32) for h in range(2)]
-        w_s = [sbuf("w_s%d" % h, [P, PASSES, HALF], U8) for h in range(2)]
+        x_raw = [sbuf("x_raw%d" % g, [P, PACK, T], F32) for g in range(PASSES)]
+        x_bf = [sbuf("x_bf%d" % g, [P, T, PACK], BF16) for g in range(PASSES)]
+        x_c = sbuf("x_c", [P, PASSES, T], U32)
+        x_s = sbuf("x_s", [P, PASSES, T], U8)
+        w_raw = [sbuf("w_raw%d" % g, [P, PACK, N], F32) for g in range(PASSES)]
+        w_bf = [sbuf("w_bf%d" % g, [P, PACK, P, PACK], BF16) for g in range(PASSES)]
+        w_c = sbuf("w_c", [P, PASSES, PACK, P], U32)
+        w_s = sbuf("w_s", [P, PASSES, PACK, P], U8)
 
-        s_sb = [sbuf("s_sb%d" % c, [P, PACK, P], F32) for c in range(CHUNKS)]
-        lo = [sbuf("lo%d" % a, [P, PACK, 2, P], F32) for a in range(2)]
-        hi = [sbuf("hi%d" % a, [P, PACK, 2, P], F32) for a in range(2)]
-        capped = [[sbuf("capped%d%d" % (h, a), [P, PACK, 2, 64], F32) for a in range(2)] for h in range(2)]
-        y_t = [[sbuf("y_t%d%d" % (h, a), [P, PACK, 2, 64], F32) for a in range(2)] for h in range(2)]
-        y_sb = [[sbuf("y_sb%d%d" % (h, a), [P, PACK, P], F32) for a in range(2)] for h in range(2)]
-        y_bf = [[sbuf("y_bf%d%d" % (h, a), [P, P, PACK], BF16) for a in range(2)] for h in range(2)]
-        y_c = [sbuf("y_c%d" % h, [P, 2, P], U32) for h in range(2)]
-        y_s = sbuf("y_s", [P, 2, 2, P], U8)
+        s_sb = sbuf("s_sb", [P, PACK, T], F32)
+        lo = sbuf("lo", [P, PACK, T], F32)
+        hi = sbuf("hi", [P, PACK, T], F32)
+        capped = sbuf("capped", [P, PACK, T], F32)
+        y_sb = [sbuf("y_sb%d" % c, [P, PACK, P], F32) for c in range(CHUNKS)]
+        y_bf = [sbuf("y_bf%d" % c, [P, P, PACK], BF16) for c in range(CHUNKS)]
+        y_c = sbuf("y_c", [P, T], U32)
+        y_s = sbuf("y_s", [P, T], U8)
 
-        nc.gpsimd.memset(wq_s[:].bitcast(I32), 0)
-        for plane in (wa_s, xq_s, wc_s):
+        nc.gpsimd.memset(wq_s_in[:].bitcast(I32), 0)
+        for plane in (wc_s_in, xq_s, wa_s_in):
             nc.vector.memset(plane[:].bitcast(I32), 0)
 
         def load_words(dst, words):
@@ -82,36 +85,28 @@ def tile_mix_three_sums_middle_pl_kernel(
                     in_=scales[:, 4 * q : 4 * q + 4, :].rearrange("g i n -> i g n").bitcast(I32),
                 )
 
-        def first_token(c):
-            return HALF * (c % 2) + P * (c // 2)
+        def load_packed_scales(plane, scales):
+            for q in range(4):
+                nc.sync.dma_start(
+                    out=plane[32 * q + 4 : 32 * q + 12].bitcast(I32),
+                    in_=scales[:, 4 * q : 4 * q + 4, :].bitcast(I32),
+                )
 
-        def load_rows(raw, src, g, col0):
-            rows = src[512 * g : 512 * (g + 1), col0 : col0 + raw.shape[2]]
-            nc.sync.dma_start(out=raw[:], in_=rows.rearrange("(p j) w -> p j w", j=PACK))
+        def load_rows(raw, src, g):
+            nc.sync.dma_start(out=raw[g][:], in_=src[512 * g : 512 * (g + 1), :].rearrange("(p j) w -> p j w", j=PACK))
 
-        def load_x(c, g):
-            load_rows(x_raw[c][g], xt, g, first_token(c))
-
-        def load_w(h, g):
-            load_rows(w_raw[h][g], wb, g, HALF * h)
-
-        load_scales(nc.gpsimd, wq_s, wq_scales)
-        make_identity(nc, ident[:])
-        load_x(0, 0)
-        load_scales(nc.sync, wa_s, wa_scales)
-        load_x(0, 1)
-        load_words(wa_c, wa_words.rearrange("g p n -> p g n"))
-        load_x(1, 0)
-        load_scales(nc.sync, xq_s, xq_scales)
-        load_x(1, 1)
+        load_scales(nc.gpsimd, wq_s_in, wq_scales)
+        load_words(wc_in, wc_words.rearrange("g p n t -> p g (n t)"))
+        load_packed_scales(wc_s_in, wc_scales)
         load_words(xq_c, xq_words.rearrange("g p n t -> p g (n t)"))
-        load_words(wc_c, wc_words.rearrange("g p n t -> p g (n t)"))
-        load_scales(nc.sync, wc_s, wc_scales)
-        load_words(wq_c, wq_words.rearrange("g p n -> p g n"))
-        for load, blocks in ((load_x, (2, 3)), (load_w, (0, 1))):
-            for i in blocks:
-                for g in range(PASSES):
-                    load(i, g)
+        load_scales(nc.sync, xq_s, xq_scales)
+        load_words(wq_in, wq_words.rearrange("g p n -> p g n"))
+        load_words(wa_in, wa_words.rearrange("g p n -> p g n"))
+        load_rows(x_raw, xt, 0)
+        load_scales(nc.sync, wa_s_in, wa_scales)
+        load_rows(x_raw, xt, 1)
+        for g in range(PASSES):
+            load_rows(w_raw, wb, g)
 
         def copy(engine, out, in_):
             if engine == "scalar":
@@ -119,212 +114,185 @@ def tile_mix_three_sums_middle_pl_kernel(
             else:
                 nc.vector.tensor_copy(out=out, in_=in_)
 
-        def round_block(engine, grouped, raw):
-            copy(engine, grouped.rearrange("p (c i) j -> p c j i", i=4), raw.rearrange("p j (c i) -> p c j i", i=4))
+        def deal(dst, src):
+            nc.vector.tensor_copy(out=dst[:], in_=src[:].rearrange("p g (m r) -> p g r m", r=PACK))
 
-        def round_x(engine, c, g):
-            round_block(engine, x_bf[c][:, g], x_raw[c][g][:])
+        def deal_fp4(dst, src):
+            nc.vector.tensor_copy(
+                out=dst[:].rearrange("p g r (m b) -> p g r m b", b=2),
+                in_=src[:].rearrange("p g (m r b) -> p g r m b", r=PACK, b=2),
+            )
 
-        def round_w(engine, h, g, b):
-            cols = slice(P * b, P * (b + 1))
-            round_block(engine, w_bf[h][g][:, cols, :], w_raw[h][g][:, :, cols])
+        def chunk(c):
+            return slice(P * c, P * (c + 1))
+
+        def interleave(engine, grouped, rows):
+            copy(engine, grouped.rearrange("p (c i) j -> p c j i", i=4), rows.rearrange("p j (c i) -> p c j i", i=4))
+
+        def round_x(engine, g, c):
+            interleave(engine, x_bf[g][:, chunk(c), :], x_raw[g][:, :, chunk(c)])
+
+        def round_w(engine, g, r0, r1):
+            copy(
+                engine,
+                w_bf[g][:, r0:r1].rearrange("p r m j -> p m j r"),
+                w_raw[g][:].rearrange("p j (m r) -> p m j r", r=PACK)[:, :, :, r0:r1],
+            )
 
         def quantize(grouped, codes, scales):
             nc.vector.quantize_mx(out=codes.bitcast(FP8X4), scales=scales, in_=grouped)
 
-        def quantize_x(c):
+        def quantize_x(g, c0, c1):
+            cols = slice(P * c0, P * c1)
+            quantize(x_bf[g][:, cols, :].rearrange("p w j -> p (w j)"), x_c[:, g, cols], x_s[:, g, cols])
+
+        def quantize_w(g, r0, r1):
             quantize(
-                x_bf[c][:].rearrange("p g w j -> p (g w j)"),
-                x_c[c][:].rearrange("p g w -> p (g w)"),
-                x_s[c][:].rearrange("p g w -> p (g w)"),
+                w_bf[g][:, r0:r1].rearrange("p r m j -> p (r m j)"),
+                w_c[:, g, r0:r1].rearrange("p r m -> p (r m)"),
+                w_s[:, g, r0:r1].rearrange("p r m -> p (r m)"),
             )
 
-        def quantize_w(h, g):
-            quantize(w_bf[h][g][:].rearrange("p w j -> p (w j)"), w_c[h][:, g, :], w_s[h][:, g, :])
+        def mx_pass(acc, w_codes, w_scales, codes, scales, g, cols, start, stop):
+            nc.tensor.matmul_mx(
+                out=acc, lhsT=w_codes, lhsT_scale=w_scales,
+                rhs=codes[:, g, cols].bitcast(FP8X4), rhs_scale=scales[:, g, cols], start=start, stop=stop,
+            )
 
-        def xq_product(acc, c, w_codes, w_dtype, w_scales, start, stop):
-            cols = slice(first_token(c), first_token(c) + P)
+        p_ps, r_ps = {}, {}
+
+        def s_product(r):
+            acc = bank("u%d" % r, "s_ps%d" % r, [P, T])
             for g in range(PASSES):
-                nc.tensor.matmul_mx(
-                    out=acc, lhsT=xq_c[:, g, cols].bitcast(FP8X4), lhsT_scale=xq_s[:, g, cols],
-                    rhs=w_codes[:, g, :].bitcast(w_dtype), rhs_scale=w_scales[:, g, :],
-                    start=start and g == 0, stop=stop and g == PASSES - 1,
+                mx_pass(
+                    acc[:], wc_c[:, g, r, :].bitcast(FP8X4), wc_s[4 * (g + 1) :, r, :],
+                    xq_c, xq_s, g, slice(0, T), g == 0, g == 1,
                 )
+            nc.scalar.copy(out=s_sb[:, r, :], in_=acc[:])
 
-        def xt_product(acc, c, w_codes, w_dtype, w_scales, start, stop):
-            for g in range(PASSES):
-                nc.tensor.matmul_mx(
-                    out=acc, lhsT=x_c[c][:, g, :].bitcast(FP8X4), lhsT_scale=x_s[c][:, g, :],
-                    rhs=w_codes[:, g, :].bitcast(w_dtype), rhs_scale=w_scales[:, g, :],
-                    start=start and g == 0, stop=stop and g == PASSES - 1,
+        def p_pass(c, w_codes, w_scales, codes, scales, g, first, last):
+            for r in range(PACK):
+                mx_pass(
+                    p_ps[c][:, r, :], w_codes[:, g, r, :].bitcast(FP4X4), w_scales[:, g, r, :],
+                    codes, scales, g, chunk(c), first and r == 0, last and r == PACK - 1,
                 )
-
-        s_ps, p_ps, r_ps = {}, {}, {}
-
-        def s_mm(c):
-            s_ps[c] = bank("u%d" % c, "s_ps%d" % c, [P, N])
-            xq_product(s_ps[c][:], c, wc_c, FP8X4, wc_s, True, True)
-
-        def s_out(engine, c):
-            copy(engine, s_sb[c][:], s_ps[c][:].rearrange("t (m r) -> t r m", r=PACK))
-
-        def p_open(c):
-            p_ps[c] = bank("v%d" % c, "p_ps%d" % c, [P, N])
-            xt_product(p_ps[c][:], c, wa_c, FP4X4, wa_s, True, False)
-
-        def p_close(c):
-            xq_product(p_ps[c][:], c, wq_c, FP4X4, wq_s, False, True)
-
-        def p_open_late(c):
-            p_ps[c] = bank("v%d" % c, "p_ps%d" % c, [P, N])
-            xq_product(p_ps[c][:], c, wq_c, FP4X4, wq_s, True, False)
-
-        def p_close_late(c):
-            xt_product(p_ps[c][:], c, wa_c, FP4X4, wa_s, False, True)
 
         def bound(dst, c, op):
             nc.vector.scalar_tensor_tensor(
-                out=dst[c // 2][:, :, c % 2, :], in0=p_ps[c][:].rearrange("t (m r) -> t r m", r=PACK),
-                scalar=P_FACTOR, in1=s_sb[c][:], op0=ALU.mult, op1=op,
+                out=dst[:, :, chunk(c)], in0=p_ps[c][:], scalar=P_FACTOR, in1=s_sb[:, :, chunk(c)],
+                op0=ALU.mult, op1=op,
             )
 
-        def r_mm(h, a, tag):
-            r_ps[h, a] = bank(tag, "r_ps%d%d" % (h, a), [P, 2, HALF])
-            for g in range(PASSES):
-                for cc in range(2):
-                    c = 2 * a + cc
-                    nc.tensor.matmul_mx(
-                        out=r_ps[h, a][:, cc, :], lhsT=x_c[c][:, g, :].bitcast(FP8X4), lhsT_scale=x_s[c][:, g, :],
-                        rhs=w_c[h][:, g, :].bitcast(FP8X4), rhs_scale=w_s[h][:, g, :],
-                        start=g == 0 and cc == 0, stop=g == PASSES - 1 and cc == 1,
+        def r_pass(g, pair):
+            for th in range(2):
+                for i in range(2):
+                    r = 2 * pair + i
+                    mx_pass(
+                        r_ps[pair, th][:, i, :], w_c[:, g, r, :].bitcast(FP8X4), w_s[:, g, r, :],
+                        x_c, x_s, g, slice(HALF * th, HALF * (th + 1)), g == 0 and i == 0, g == 1 and i == 1,
                     )
 
-        def cap(h, a, rows):
+        def cap(pair, c):
+            rows = slice(2 * pair, 2 * pair + 2)
             nc.vector.tensor_tensor(
-                out=capped[h][a][:, rows], in0=r_ps[h, a][:].rearrange("t c (m r) -> t r c m", r=PACK)[:, rows],
-                in1=hi[a][:, rows, :, 64 * h : 64 * (h + 1)], op=ALU.min,
+                out=capped[:, rows, chunk(c)], in0=r_ps[pair, c // 2][:, :, chunk(c % 2)],
+                in1=hi[:, rows, chunk(c)], op=ALU.min,
             )
 
-        def floor(h, a, rows):
+        def floor(pair, c):
+            rows = slice(2 * pair, 2 * pair + 2)
             nc.vector.tensor_tensor(
-                out=y_t[h][a][:, rows], in0=capped[h][a][:, rows],
-                in1=lo[a][:, rows, :, 64 * h : 64 * (h + 1)], op=ALU.max,
+                out=y_sb[c][:, rows, :], in0=capped[:, rows, chunk(c)], in1=lo[:, rows, chunk(c)], op=ALU.max,
             )
 
-        def clamp(h, a):
-            for step in (cap, floor):
-                for r0 in (0, 2):
-                    step(h, a, slice(r0, r0 + 2))
+        def store_values(c):
+            nc.sync.dma_start(out=out_0[:, chunk(c)].rearrange("(p r) t -> p r t", r=PACK), in_=y_sb[c][:])
 
-        def turn(h, a, tag):
-            turned = bank(tag, "t_ps%d%d%s" % (h, a, tag), [P, PACK, P])
-            for r in range(PACK):
-                nc.tensor.transpose(turned[:, r, :], y_t[h][a][:, r].rearrange("t c m -> t (c m)"), ident[:])
-            return turned
+        def y_round(engine, c):
+            interleave(engine, y_bf[c][:], y_sb[c][:])
 
-        def y_out(turned, h, a):
-            nc.scalar.copy(out=y_sb[h][a][:], in_=turned[:])
+        def y_quantize(c):
+            quantize(y_bf[c][:].rearrange("p t r -> p (t r)"), y_c[:, chunk(c)], y_s[:, chunk(c)])
 
-        def y_round(engine, turned, h, a):
-            copy(engine, y_bf[h][a][:], turned[:].rearrange("p r t -> p t r"))
-
-        def y_quantize(h, a):
-            quantize(y_bf[h][a][:].rearrange("p t r -> p (t r)"), y_c[h][:, a, :], y_s[:, h, a, :])
-
-        def store_values(queue, h, a):
-            for cc in range(2):
-                t0 = first_token(2 * a + cc)
-                rows = out_0[HALF * h : HALF * (h + 1), t0 : t0 + P]
-                queue.dma_start(out=rows.rearrange("(p r) t -> p r t", r=PACK), in_=y_sb[h][a][64 * cc : 64 * (cc + 1)])
-
-        def store_words(h):
+        def store_words(queue, c0, c1):
+            cols = slice(P * c0, P * c1)
             words = out_1[0].rearrange("p t r -> p (t r)").bitcast(I32)
-            for cc in range(2):
-                nc.sync.dma_start(
-                    out=words[64 * h : 64 * (h + 1), HALF * cc : HALF * (cc + 1)],
-                    in_=y_c[h][64 * cc : 64 * (cc + 1)].rearrange("p a t -> p (a t)").bitcast(I32),
-                )
+            queue.dma_start(out=words[:, cols], in_=y_c[:, cols].bitcast(I32))
 
         def store_scales():
-            rows = out_2[0].rearrange("(h b i) t -> b i h t", h=2, b=2)
             for q in range(4):
-                cc, b = divmod(q, 2)
-                (nc.sync, nc.scalar)[b].dma_start(
-                    out=rows[b][:, :, HALF * cc : HALF * (cc + 1)].bitcast(I32),
-                    in_=y_s[32 * q : 32 * q + 4].rearrange("i h a t -> i h (a t)").bitcast(I32),
+                (nc.scalar, nc.sync)[q == 3].dma_start(
+                    out=out_2[0, 4 * q : 4 * q + 4, :].bitcast(I32), in_=y_s[32 * q : 32 * q + 4, :].bitcast(I32)
                 )
 
-        def post(h, a):
-            turned = turn(h, a, "v%d" % (2 * h + a))
-            y_out(turned, h, a)
-            store_values(nc.sync, h, a)
-            y_round(S, turned, h, a)
-
         S, V = "scalar", "vector"
+        deal(wc_c, wc_in)
+        nc.vector.tensor_copy(out=wc_s[:], in_=wc_s_in[:].rearrange("p (m r) -> p r m", r=PACK))
+        for r in range(PACK):
+            s_product(r)
+        deal(wq_s, wq_s_in)
+        deal_fp4(wq_c, wq_in)
+        deal_fp4(wa_c, wa_in)
+        deal(wa_s, wa_s_in)
+        for c in range(CHUNKS):
+            p_ps[c] = bank("v%d" % c, "p_ps%d" % c, [P, PACK, P])
         for c in range(2):
-            round_x(S, c, 0)
-            round_x(V, c, 1)
-            quantize_x(c)
-            p_open(c)
-        s_mm(0)
-        s_out(S, 0)
-        round_x(V, 2, 0)
-        p_close(0)
-        s_mm(1)
-        p_close(1)
-        round_x(S, 2, 1)
-        s_out(S, 1)
-        bound(hi, 0, ALU.max)
-        bound(lo, 0, ALU.min)
-        quantize_x(2)
-        s_mm(2)
-        p_open_late(2)
-        p_close_late(2)
-        round_x(S, 3, 0)
-        s_out(S, 2)
-        round_x(S, 3, 1)
-        bound(hi, 1, ALU.max)
-        bound(lo, 1, ALU.min)
-        bound(hi, 2, ALU.max)
-        quantize_x(3)
-        s_mm(3)
-        p_open_late(3)
-        p_close_late(3)
-        s_out(S, 3)
-        bound(lo, 2, ALU.min)
-        round_w(V, 0, 0, 0)
-        round_w(S, 0, 0, 1)
-        round_w(S, 0, 1, 0)
-        round_w(S, 0, 1, 1)
-        bound(hi, 3, ALU.max)
-        quantize_w(0, 0)
-        quantize_w(0, 1)
-        r_mm(0, 0, "u0")
-        r_mm(0, 1, "u1")
-        bound(lo, 3, ALU.min)
-        for g in range(PASSES):
-            for b in range(2):
-                round_w(S, 1, g, b)
-        clamp(0, 0)
-        post(0, 0)
-        for g in range(PASSES):
-            quantize_w(1, g)
-        r_mm(1, 0, "u2")
-        r_mm(1, 1, "u3")
-        clamp(0, 1)
-        post(0, 1)
-        clamp(1, 0)
-        post(1, 0)
-        clamp(1, 1)
-        last_for_planes = turn(1, 1, "v3")
-        last_for_values = turn(1, 1, "u0")
-        y_quantize(0, 0)
-        y_quantize(0, 1)
-        store_words(0)
-        y_round(V, last_for_planes, 1, 1)
-        y_out(last_for_values, 1, 1)
-        store_values(nc.scalar, 1, 1)
-        y_quantize(1, 0)
-        y_quantize(1, 1)
-        store_words(1)
+            for g in range(PASSES):
+                p_pass(c, wq_c, wq_s, xq_c, xq_s, g, g == 0, False)
+        for c in range(CHUNKS):
+            round_x(S if c < 2 else V, 0, c)
+        quantize_x(0, 0, CHUNKS)
+        for c in range(CHUNKS):
+            round_x(V if c == 0 else S, 1, c)
+        for c in range(2):
+            p_pass(c, wa_c, wa_s, x_c, x_s, 0, False, False)
+            quantize_x(1, c, c + 1)
+            p_pass(c, wa_c, wa_s, x_c, x_s, 1, False, True)
+        round_w(S, 0, 0, PACK)
+        for pair in range(2):
+            round_w(S, 1, 2 * pair, 2 * pair + 2)
+        for pair in range(2):
+            for th in range(2):
+                r_ps[pair, th] = bank("u%d" % (2 * pair + th), "r_ps%d%d" % (pair, th), [P, 2, HALF])
+        for c in range(CHUNKS):
+            bound(hi, c, ALU.max)
+            if c < 2:
+                quantize_x(1, c + 2, c + 3)
+                p_pass(c + 2, wa_c, wa_s, x_c, x_s, 1, True, False)
+                p_pass(c + 2, wa_c, wa_s, x_c, x_s, 0, False, False)
+                for g in range(PASSES):
+                    p_pass(c + 2, wq_c, wq_s, xq_c, xq_s, g, False, g == 1)
+            elif c == 2:
+                quantize_w(0, 0, PACK)
+                r_pass(0, 0)
+            else:
+                quantize_w(1, 0, 2)
+                r_pass(1, 0)
+                r_pass(0, 1)
+            bound(lo, c, ALU.min)
+
+        quantize_w(1, 2, PACK)
+        r_pass(1, 1)
+        for step in (cap, floor):
+            for c in range(2):
+                step(0, c)
+        for step in (cap, floor):
+            for c in range(2):
+                step(1, c)
+        for c in range(2):
+            store_values(c)
+            y_round(S, c)
+        for c in range(2, CHUNKS):
+            for pair in range(2):
+                cap(pair, c)
+            y_quantize(c - 2)
+            for pair in range(2):
+                floor(pair, c)
+            store_values(c)
+        y_round(S, 2)
+        y_quantize(2)
+        store_words(nc.scalar, 0, 3)
+        y_round(V, 3)
+        y_quantize(3)
+        store_words(nc.sync, 3, CHUNKS)
         store_scales()

@@ -95,12 +95,12 @@ def tile_mix_three_sums_middle_pl_kernel(
         def load_rows(raw, src, g):
             nc.sync.dma_start(out=raw[g][:], in_=src[512 * g : 512 * (g + 1), :].rearrange("(p j) w -> p j w", j=PACK))
 
-        load_scales(nc.gpsimd, wq_s_in, wq_scales)
         load_words(wc_in, wc_words.rearrange("g p n t -> p g (n t)"))
         load_packed_scales(wc_s_in, wc_scales)
         load_words(xq_c, xq_words.rearrange("g p n t -> p g (n t)"))
         load_scales(nc.sync, xq_s, xq_scales)
         load_words(wq_in, wq_words.rearrange("g p n -> p g n"))
+        load_scales(nc.sync, wq_s_in, wq_scales)
         load_words(wa_in, wa_words.rearrange("g p n -> p g n"))
         load_rows(x_raw, xt, 0)
         load_scales(nc.sync, wa_s_in, wa_scales)

@@ -79,11 +79,9 @@ def tile_mix_three_sums_middle_pl_kernel(
             nc.sync.dma_start(out=dst[:].bitcast(I32), in_=words.bitcast(I32))
 
         def load_scales(queue, plane, scales):
-            for q in range(4):
-                queue.dma_start(
-                    out=plane[32 * q : 32 * q + 4].bitcast(I32),
-                    in_=scales[:, 4 * q : 4 * q + 4, :].rearrange("g i n -> i g n").bitcast(I32),
-                )
+            rows = scales.rearrange("g (q i) n -> i q g n", i=4)
+            for i in range(4):
+                queue.dma_start(out=plane[i:P:32].bitcast(I32), in_=rows[i].bitcast(I32))
 
         def load_packed_scales(plane, scales):
             for q in range(4):
@@ -100,8 +98,8 @@ def tile_mix_three_sums_middle_pl_kernel(
         load_words(xq_c, xq_words.rearrange("g p n t -> p g (n t)"))
         load_scales(nc.sync, xq_s, xq_scales)
         load_words(wq_in, wq_words.rearrange("g p n -> p g n"))
-        load_scales(nc.sync, wq_s_in, wq_scales)
         load_words(wa_in, wa_words.rearrange("g p n -> p g n"))
+        load_scales(nc.sync, wq_s_in, wq_scales)
         load_rows(x_raw, xt, 0)
         load_scales(nc.sync, wa_s_in, wa_scales)
         load_rows(x_raw, xt, 1)
@@ -220,32 +218,34 @@ def tile_mix_three_sums_middle_pl_kernel(
             queue.dma_start(out=words[:, cols], in_=y_c[:, cols].bitcast(I32))
 
         def store_scales():
-            for q in range(4):
-                (nc.scalar, nc.sync)[q == 3].dma_start(
-                    out=out_2[0, 4 * q : 4 * q + 4, :].bitcast(I32), in_=y_s[32 * q : 32 * q + 4, :].bitcast(I32)
-                )
+            rows = out_2[0].rearrange("(q i) t -> i q t", i=4)
+            for i in range(4):
+                (nc.sync, nc.scalar)[i % 2].dma_start(out=rows[i].bitcast(I32), in_=y_s[i:P:32, :].bitcast(I32))
 
         S, V = "scalar", "vector"
         deal(wc_c, wc_in)
         nc.vector.tensor_copy(out=wc_s[:], in_=wc_s_in[:].rearrange("p (m r) -> p r m", r=PACK))
         for r in range(PACK):
             s_product(r)
-        deal(wq_s, wq_s_in)
         deal_fp4(wq_c, wq_in)
+        deal(wq_s, wq_s_in)
         deal_fp4(wa_c, wa_in)
         deal(wa_s, wa_s_in)
         for c in range(CHUNKS):
             p_ps[c] = bank("v%d" % c, "p_ps%d" % c, [P, PACK, P])
-        for c in range(2):
+        last = CHUNKS - 1
+        for c in range(last):
             for g in range(PASSES):
                 p_pass(c, wq_c, wq_s, xq_c, xq_s, g, g == 0, False)
         for c in range(CHUNKS):
-            round_x(S if c < 2 else V, 0, c)
-        quantize_x(0, 0, CHUNKS)
+            round_x(S if c < last else V, 0, c)
         for c in range(CHUNKS):
-            round_x(V if c == 0 else S, 1, c)
-        for c in range(2):
-            p_pass(c, wa_c, wa_s, x_c, x_s, 0, False, False)
+            quantize_x(0, c, c + 1)
+            if c < last:
+                p_pass(c, wa_c, wa_s, x_c, x_s, 0, False, False)
+        for c in range(CHUNKS):
+            round_x(S if c % 2 else V, 1, c)
+        for c in range(last):
             quantize_x(1, c, c + 1)
             p_pass(c, wa_c, wa_s, x_c, x_s, 1, False, True)
         round_w(S, 0, 0, PACK)
@@ -256,20 +256,20 @@ def tile_mix_three_sums_middle_pl_kernel(
                 r_ps[pair, th] = bank("u%d" % (2 * pair + th), "r_ps%d%d" % (pair, th), [P, 2, HALF])
         for c in range(CHUNKS):
             bound(hi, c, ALU.max)
-            if c < 2:
-                quantize_x(1, c + 2, c + 3)
-                p_pass(c + 2, wa_c, wa_s, x_c, x_s, 1, True, False)
-                p_pass(c + 2, wa_c, wa_s, x_c, x_s, 0, False, False)
+            if c == 0:
+                quantize_x(1, last, CHUNKS)
+                p_pass(last, wa_c, wa_s, x_c, x_s, 1, True, False)
+                p_pass(last, wa_c, wa_s, x_c, x_s, 0, False, False)
                 for g in range(PASSES):
-                    p_pass(c + 2, wq_c, wq_s, xq_c, xq_s, g, False, g == 1)
-            elif c == 2:
-                quantize_w(0, 0, PACK)
-                r_pass(0, 0)
-            else:
+                    p_pass(last, wq_c, wq_s, xq_c, xq_s, g, False, g == 1)
+            elif c == last:
                 quantize_w(1, 0, 2)
                 r_pass(1, 0)
                 r_pass(0, 1)
             bound(lo, c, ALU.min)
+            if c == 2:
+                quantize_w(0, 0, PACK)
+                r_pass(0, 0)
 
         quantize_w(1, 2, PACK)
         r_pass(1, 1)
@@ -286,13 +286,14 @@ def tile_mix_three_sums_middle_pl_kernel(
             for pair in range(2):
                 cap(pair, c)
             y_quantize(c - 2)
+            if c == last:
+                store_words(nc.sync, 0, 2)
             for pair in range(2):
                 floor(pair, c)
             store_values(c)
         y_round(S, 2)
         y_quantize(2)
-        store_words(nc.scalar, 0, 3)
-        y_round(V, 3)
-        y_quantize(3)
-        store_words(nc.sync, 3, CHUNKS)
+        y_round(V, last)
+        y_quantize(last)
+        store_words(nc.scalar, 2, CHUNKS)
         store_scales()

from contextlib import ExitStack

import concourse.mybir as mybir

K, L, T, N = 1024, 1024, 512, 512
FLOPS = 2 * N * T * (2 * K + 2 * L)

F32 = mybir.dt.float32
BF16 = mybir.dt.bfloat16
I32 = mybir.dt.int32
U32 = mybir.dt.uint32
U8 = mybir.dt.uint8
FP8X4 = mybir.dt.float8_e4m3fn_x4
FP4X4 = mybir.dt.float4_e2m1fn_x4
ALU = mybir.AluOpType

P = 128
PACK = 4
PASSES = 2
CHUNKS = 4
HALF = 256
P_FACTOR = 0.7


def tile_mix_three_sums_middle_pl_kernel(
    tc, xt, wa_words, wa_scales, xq_words, xq_scales, wq_words, wq_scales, wb, wc_words, wc_scales,
    out_0, out_1, out_2,
):
    nc = tc.nc
    with ExitStack() as ctx:
        sb = ctx.enter_context(tc.tile_pool(name="sb", bufs=1))
        ps = ctx.enter_context(tc.psum_pool(name="ps", bufs=1))
        ctx.enter_context(tc.manual_schedule())

        def sbuf(name, shape, dtype):
            return sb.tile(shape, dtype, name=name, align_bytes=64)

        def bank(tag, name, shape):
            return ps.tile(shape, F32, name=name, tag=tag)

        wc_in = sbuf("wc_in", [P, PASSES, N], I32)
        wq_in = sbuf("wq_in", [P, PASSES, 2 * N], U8)
        wa_in = sbuf("wa_in", [P, PASSES, 2 * N], U8)
        wc_s_in = sbuf("wc_s_in", [P, N], U8)
        wq_s_in = sbuf("wq_s_in", [P, PASSES, N], U8)
        wa_s_in = sbuf("wa_s_in", [P, PASSES, N], U8)
        wc_c = sbuf("wc_c", [P, PASSES, PACK, P], I32)
        wq_c = sbuf("wq_c", [P, PASSES, PACK, 2 * P], U8)
        wa_c = sbuf("wa_c", [P, PASSES, PACK, 2 * P], U8)
        wc_s = sbuf("wc_s", [P, PACK, P], U8)
        wq_s = sbuf("wq_s", [P, PASSES, PACK, P], U8)
        wa_s = sbuf("wa_s", [P, PASSES, PACK, P], U8)
        xq_c = sbuf("xq_c", [P, PASSES, T], I32)
        xq_s = sbuf("xq_s", [P, PASSES, T], U8)

        x_raw = [sbuf("x_raw%d" % g, [P, PACK, T], F32) for g in range(PASSES)]
        x_bf = [sbuf("x_bf%d" % g, [P, T, PACK], BF16) for g in range(PASSES)]
        x_c = sbuf("x_c", [P, PASSES, T], U32)
        x_s = sbuf("x_s", [P, PASSES, T], U8)
        w_raw = [sbuf("w_raw%d" % g, [P, PACK, N], F32) for g in range(PASSES)]
        w_bf = [sbuf("w_bf%d" % g, [P, PACK, P, PACK], BF16) for g in range(PASSES)]
        w_c = sbuf("w_c", [P, PASSES, PACK, P], U32)
        w_s = sbuf("w_s", [P, PASSES, PACK, P], U8)

        s_sb = sbuf("s_sb", [P, PACK, T], F32)
        lo = sbuf("lo", [P, PACK, T], F32)
        hi = sbuf("hi", [P, PACK, T], F32)
        capped = sbuf("capped", [P, PACK, T], F32)
        y_sb = [sbuf("y_sb%d" % c, [P, PACK, P], F32) for c in range(CHUNKS)]
        y_bf = [sbuf("y_bf%d" % c, [P, P, PACK], BF16) for c in range(CHUNKS)]
        y_c = sbuf("y_c", [P, T], U32)
        y_s = sbuf("y_s", [P, T], U8)

        nc.gpsimd.memset(wq_s_in[:].bitcast(I32), 0)
        for plane in (wc_s_in, xq_s, wa_s_in):
            nc.vector.memset(plane[:].bitcast(I32), 0)

        def load_words(dst, words):
            nc.sync.dma_start(out=dst[:].bitcast(I32), in_=words.bitcast(I32))

        def load_scales(queue, plane, scales):
            rows = scales.rearrange("g (q i) n -> i q g n", i=4)
            for i in range(4):
                queue.dma_start(out=plane[i:P:32].bitcast(I32), in_=rows[i].bitcast(I32))

        def load_packed_scales(plane, scales):
            for q in range(4):
                nc.sync.dma_start(
                    out=plane[32 * q + 4 : 32 * q + 12].bitcast(I32),
                    in_=scales[:, 4 * q : 4 * q + 4, :].bitcast(I32),
                )

        def load_rows(raw, src, g):
            nc.sync.dma_start(out=raw[g][:], in_=src[512 * g : 512 * (g + 1), :].rearrange("(p j) w -> p j w", j=PACK))

        load_words(wc_in, wc_words.rearrange("g p n t -> p g (n t)"))
        load_packed_scales(wc_s_in, wc_scales)
        load_words(xq_c, xq_words.rearrange("g p n t -> p g (n t)"))
        load_scales(nc.sync, xq_s, xq_scales)
        load_words(wq_in, wq_words.rearrange("g p n -> p g n"))
        load_words(wa_in, wa_words.rearrange("g p n -> p g n"))
        load_scales(nc.sync, wq_s_in, wq_scales)
        load_rows(x_raw, xt, 0)
        load_scales(nc.sync, wa_s_in, wa_scales)
        load_rows(x_raw, xt, 1)
        for g in range(PASSES):
            load_rows(w_raw, wb, g)

        def copy(engine, out, in_):
            if engine == "scalar":
                nc.scalar.copy(out=out, in_=in_)
            else:
                nc.vector.tensor_copy(out=out, in_=in_)

        def deal(dst, src):
            nc.vector.tensor_copy(out=dst[:], in_=src[:].rearrange("p g (m r) -> p g r m", r=PACK))

        def deal_fp4(dst, src):
            nc.vector.tensor_copy(
                out=dst[:].rearrange("p g r (m b) -> p g r m b", b=2),
                in_=src[:].rearrange("p g (m r b) -> p g r m b", r=PACK, b=2),
            )

        def chunk(c):
            return slice(P * c, P * (c + 1))

        def interleave(engine, grouped, rows):
            copy(engine, grouped.rearrange("p (c i) j -> p c j i", i=4), rows.rearrange("p j (c i) -> p c j i", i=4))

        def round_x(engine, g, c):
            interleave(engine, x_bf[g][:, chunk(c), :], x_raw[g][:, :, chunk(c)])

        def round_w(engine, g, r0, r1):
            copy(
                engine,
                w_bf[g][:, r0:r1].rearrange("p r m j -> p m j r"),
                w_raw[g][:].rearrange("p j (m r) -> p m j r", r=PACK)[:, :, :, r0:r1],
            )

        def quantize(grouped, codes, scales):
            nc.vector.quantize_mx(out=codes.bitcast(FP8X4), scales=scales, in_=grouped)

        def quantize_x(g, c0, c1):
            cols = slice(P * c0, P * c1)
            quantize(x_bf[g][:, cols, :].rearrange("p w j -> p (w j)"), x_c[:, g, cols], x_s[:, g, cols])

        def quantize_w(g, r0, r1):
            quantize(
                w_bf[g][:, r0:r1].rearrange("p r m j -> p (r m j)"),
                w_c[:, g, r0:r1].rearrange("p r m -> p (r m)"),
                w_s[:, g, r0:r1].rearrange("p r m -> p (r m)"),
            )

        def mx_pass(acc, w_codes, w_scales, codes, scales, g, cols, start, stop):
            nc.tensor.matmul_mx(
                out=acc, lhsT=w_codes, lhsT_scale=w_scales,
                rhs=codes[:, g, cols].bitcast(FP8X4), rhs_scale=scales[:, g, cols], start=start, stop=stop,
            )

        p_ps, r_ps = {}, {}

        def s_product(r):
            acc = bank("u%d" % r, "s_ps%d" % r, [P, T])
            for g in range(PASSES):
                mx_pass(
                    acc[:], wc_c[:, g, r, :].bitcast(FP8X4), wc_s[4 * (g + 1) :, r, :],
                    xq_c, xq_s, g, slice(0, T), g == 0, g == 1,
                )
            nc.scalar.copy(out=s_sb[:, r, :], in_=acc[:])

        def p_pass(c, w_codes, w_scales, codes, scales, g, first, last):
            for r in range(PACK):
                mx_pass(
                    p_ps[c][:, r, :], w_codes[:, g, r, :].bitcast(FP4X4), w_scales[:, g, r, :],
                    codes, scales, g, chunk(c), first and r == 0, last and r == PACK - 1,
                )

        def bound(dst, c, op):
            nc.vector.scalar_tensor_tensor(
                out=dst[:, :, chunk(c)], in0=p_ps[c][:], scalar=P_FACTOR, in1=s_sb[:, :, chunk(c)],
                op0=ALU.mult, op1=op,
            )

        def r_pass(g, pair):
            for th in range(2):
                for i in range(2):
                    r = 2 * pair + i
                    mx_pass(
                        r_ps[pair, th][:, i, :], w_c[:, g, r, :].bitcast(FP8X4), w_s[:, g, r, :],
                        x_c, x_s, g, slice(HALF * th, HALF * (th + 1)), g == 0 and i == 0, g == 1 and i == 1,
                    )

        def cap(pair, c):
            rows = slice(2 * pair, 2 * pair + 2)
            nc.vector.tensor_tensor(
                out=capped[:, rows, chunk(c)], in0=r_ps[pair, c // 2][:, :, chunk(c % 2)],
                in1=hi[:, rows, chunk(c)], op=ALU.min,
            )

        def floor(pair, c):
            rows = slice(2 * pair, 2 * pair + 2)
            nc.vector.tensor_tensor(
                out=y_sb[c][:, rows, :], in0=capped[:, rows, chunk(c)], in1=lo[:, rows, chunk(c)], op=ALU.max,
            )

        def store_values(c):
            nc.sync.dma_start(out=out_0[:, chunk(c)].rearrange("(p r) t -> p r t", r=PACK), in_=y_sb[c][:])

        def y_round(engine, c):
            interleave(engine, y_bf[c][:], y_sb[c][:])

        def y_quantize(c):
            quantize(y_bf[c][:].rearrange("p t r -> p (t r)"), y_c[:, chunk(c)], y_s[:, chunk(c)])

        def store_words(queue, c0, c1):
            cols = slice(P * c0, P * c1)
            words = out_1[0].rearrange("p t r -> p (t r)").bitcast(I32)
            queue.dma_start(out=words[:, cols], in_=y_c[:, cols].bitcast(I32))

        def store_scales():
            rows = out_2[0].rearrange("(q i) t -> i q t", i=4)
            for i in range(4):
                (nc.sync, nc.scalar)[i % 2].dma_start(out=rows[i].bitcast(I32), in_=y_s[i:P:32, :].bitcast(I32))

        S, V = "scalar", "vector"
        deal(wc_c, wc_in)
        nc.vector.tensor_copy(out=wc_s[:], in_=wc_s_in[:].rearrange("p (m r) -> p r m", r=PACK))
        for r in range(PACK):
            s_product(r)
        deal_fp4(wq_c, wq_in)
        deal(wq_s, wq_s_in)
        deal_fp4(wa_c, wa_in)
        deal(wa_s, wa_s_in)
        for c in range(CHUNKS):
            p_ps[c] = bank("v%d" % c, "p_ps%d" % c, [P, PACK, P])
        last = CHUNKS - 1
        for c in range(last):
            for g in range(PASSES):
                p_pass(c, wq_c, wq_s, xq_c, xq_s, g, g == 0, False)
        for c in range(CHUNKS):
            round_x(S if c < last else V, 0, c)
        for c in range(CHUNKS):
            quantize_x(0, c, c + 1)
            if c < last:
                p_pass(c, wa_c, wa_s, x_c, x_s, 0, False, False)
        for c in range(CHUNKS):
            round_x(S if c % 2 else V, 1, c)
        for c in range(last):
            quantize_x(1, c, c + 1)
            p_pass(c, wa_c, wa_s, x_c, x_s, 1, False, True)
        round_w(S, 0, 0, PACK)
        for pair in range(2):
            round_w(S, 1, 2 * pair, 2 * pair + 2)
        for pair in range(2):
            for th in range(2):
                r_ps[pair, th] = bank("u%d" % (2 * pair + th), "r_ps%d%d" % (pair, th), [P, 2, HALF])
        for c in range(CHUNKS):
            bound(hi, c, ALU.max)
            if c == 0:
                quantize_x(1, last, CHUNKS)
                p_pass(last, wa_c, wa_s, x_c, x_s, 1, True, False)
                p_pass(last, wa_c, wa_s, x_c, x_s, 0, False, False)
                for g in range(PASSES):
                    p_pass(last, wq_c, wq_s, xq_c, xq_s, g, False, g == 1)
            elif c == last:
                quantize_w(1, 0, 2)
                r_pass(1, 0)
                r_pass(0, 1)
            bound(lo, c, ALU.min)
            if c == 2:
                quantize_w(0, 0, PACK)
                r_pass(0, 0)

        quantize_w(1, 2, PACK)
        r_pass(1, 1)
        for step in (cap, floor):
            for c in range(2):
                step(0, c)
        for step in (cap, floor):
            for c in range(2):
                step(1, c)
        for c in range(2):
            store_values(c)
            y_round(S, c)
        for c in range(2, CHUNKS):
            for pair in range(2):
                cap(pair, c)
            y_quantize(c - 2)
            if c == last:
                store_words(nc.sync, 0, 2)
            for pair in range(2):
                floor(pair, c)
            store_values(c)
        y_round(S, 2)
        y_quantize(2)
        y_round(V, last)
        y_quantize(last)
        store_words(nc.scalar, 2, CHUNKS)
        store_scales()
